import numpy as np
import ml_dtypes


def mxq(x, axis, fmt="e4m3"):
    dtype, down = {"e4m3": (ml_dtypes.float8_e4m3fn, 7), "e5m2": (ml_dtypes.float8_e5m2, 14)}[fmt]
    v = np.moveaxis(np.asarray(x, np.float32).astype(ml_dtypes.bfloat16).astype(np.float64), axis, -1)
    blocks = v.reshape(v.shape[:-1] + (-1, 32))
    amax = np.abs(blocks).max(-1, keepdims=True)
    byte = np.maximum(np.where(amax > 0, np.frexp(amax)[1] - 1 + 127, 0) - down, 1)
    scale = np.exp2(byte - 127.0)
    codes = (blocks / scale).astype(np.float32).astype(dtype).astype(np.float64)
    return np.moveaxis((codes * scale).reshape(v.shape), -1, axis)


WIDE = False


def mx_kscale(k):
    if not WIDE:
        return np.ones(k)
    levels = np.array([10, -10, 5, -5, 0])
    if k % 512:
        return np.exp2(np.random.permutation(np.resize(levels, k // 32))).repeat(32)
    a = np.empty((k // 512, 16))
    for p in range(k // 512):
        a[p, :8] = np.random.permutation(np.resize(levels, 8))
        for g in range(8):
            far = levels[np.abs(levels - a[p, g]) >= 10]
            a[p, g + 8] = far[np.random.randint(len(far))]
    return np.exp2(a.ravel()).repeat(32)


def f64(x):
    return np.asarray(x).astype(np.float64)


def striped(idx):
    return np.tile(idx.reshape(-1, 16).T, (8, 1)).astype(np.uint16)


def unstriped(offs):
    return offs[:16].T.reshape(-1).astype(np.int64)


def pack_weight(w):
    k, n = w.shape
    w = f64(np.asarray(w, np.float32).astype(ml_dtypes.bfloat16)).reshape(k // 32, 32, n)
    amax = np.abs(w).max(1)
    byte = np.clip(np.where(amax > 0, np.frexp(amax)[1] - 1 + 127 - 7, 1), 1, 254)
    scaled = (w * np.exp2(127.0 - byte)[:, None, :]).reshape(k, n).astype(np.float32)
    words = np.ascontiguousarray(scaled.reshape(k // 512, 128, 4, n).transpose(0, 1, 3, 2)).astype(ml_dtypes.float8_e4m3fn).view(np.uint8)
    return words, np.ascontiguousarray(byte.astype(np.uint8).reshape(k // 512, 16, n))


def unpack_weight(words, scales):
    g, p, n, _ = words.shape
    vals = np.ascontiguousarray(words).view(ml_dtypes.float8_e4m3fn).astype(np.float64) * np.repeat(np.exp2(scales.astype(np.float64) - 127.0), 8, axis=1)[..., None]
    return vals.transpose(0, 1, 3, 2).reshape(g * 512, n)


K, T, S, H, Z, W = 512, 2048, 512, 512, 512, 2048


def setup_inputs():
    n = np.random.standard_normal
    s = mx_kscale(K)[:, None]
    u = mx_kscale(H)
    packed_xT = pack_weight(n((K, T)) * s)
    packed_eT = pack_weight(n((K, W)) * s)
    return {
        "x_words": packed_xT[0],
        "x_scales": packed_xT[1],
        "w1": (n((K, H)) / np.sqrt(K) / s).astype(np.float32),
        "e_words": packed_eT[0],
        "e_scales": packed_eT[1],
        "w2": (n((K, H)) / np.sqrt(K) / s).astype(np.float32),
        "w3": (n((K, H)) / np.sqrt(K) / s).astype(np.float32),
        "unit": (np.random.uniform(0.6, 1.4, (H, 1)) * u[:, None]).astype(np.float32),
        "unit2": (np.random.uniform(0.6, 1.4, (H, 1)) / np.sqrt(H) / u[:, None]).astype(np.float32),
        "offs": striped(np.random.permutation(T)[:S]),
        "gal": striped(np.random.permutation(W)[:Z]),
        "cam": striped(np.random.permutation(Z)),
        "nn1": striped(np.random.permutation(Z)),
        "nn2": striped(np.random.permutation(Z)),
    }


def reference(x_words, x_scales, w1, e_words, e_scales, w2, w3, unit, unit2, offs, gal, cam, nn1, nn2):
    xq = unpack_weight(x_words, x_scales)[:, unstriped(offs)]
    y = mxq(f64(w1), 0, "e4m3").T @ xq
    pb = np.tanh(y)
    hid = f64(unit) * pb
    e_gal = unpack_weight(e_words, e_scales)[:, unstriped(gal)]
    ye = mxq(f64(w2), 0, "e4m3").T @ e_gal
    yg = mxq(f64(w3), 0, "e4m3").T @ e_gal
    gc = yg[:, unstriped(cam)]
    aug = ye + 0.5 * gc
    hid2 = f64(unit2) * aug
    sc = mxq(hid, 0, "e4m3").T @ mxq(hid2, 0, "e4m3")
    s1 = sc[:, unstriped(nn1)]
    s2 = sc[:, unstriped(nn2)]
    return 0.5 * sc + np.minimum(s1, s2)

@@ -1,0 +1,239 @@
+from contextlib import ExitStack
+
+import concourse.mybir as mybir
+from concourse.masks import make_identity
+
+K, T, S, H, Z = 512, 2048, 512, 512, 512
+FLOPS = 2 * K * H * S + 2 * 2 * K * H * Z + 2 * H * S * Z
+
+F32 = mybir.dt.float32
+BF16 = mybir.dt.bfloat16
+I32 = mybir.dt.int32
+U32 = mybir.dt.uint32
+U16 = mybir.dt.uint16
+U8 = mybir.dt.uint8
+FP8X4 = mybir.dt.float8_e4m3fn_x4
+ALU = mybir.AluOpType
+ACT = mybir.ActivationFunctionType
+
+P = 128
+PACK = 4
+WINDOW = 528
+NN2_ON_VECTOR = 384
+WEAVE_ON_VECTOR = 320
+
+
+def tile_picked_yreidr_min_p_kernel(
+    tc, x_words, x_scales, w1, e_words, e_scales, w2, w3, unit, unit2, offs, gal, cam, nn1, nn2, out
+):
+    nc = tc.nc
+    with ExitStack() as ctx:
+        sb = ctx.enter_context(tc.tile_pool(name="sb", bufs=1))
+        psum = ctx.enter_context(tc.psum_pool(name="psum", bufs=1))
+
+        def load_list(src, name):
+            lst = sb.tile([P, src.shape[1]], U16, name=name)
+            nc.sync.dma_start(lst[:], src)
+            return lst
+
+        def load_weight(src, name):
+            raw = sb.tile([P, PACK, H], F32, name=name)
+            nc.sync.dma_start(raw[:], src.rearrange("(p j) c -> p j c", j=PACK))
+            return raw
+
+        def load_words(src, name):
+            table = sb.tile([P, T], U32, name=name)
+            nc.sync.dma_start(table[:].bitcast(I32), src[0].rearrange("p n t -> p (n t)").bitcast(I32))
+            return table
+
+        def load_scales(src, name):
+            table = sb.tile([P, T], U8, name=name)
+            nc.vector.memset(table[:].bitcast(I32), 0)
+            for q in range(4):
+                nc.sync.dma_start(table[32 * q : 32 * q + 4, :].bitcast(I32), src[0, 4 * q : 4 * q + 4, :].bitcast(I32))
+            return table
+
+        def load_factors():
+            rows = sb.tile([P, P], F32, name="factor_rows")
+            nc.vector.memset(rows[:], 0.0)
+            for place, src in enumerate((unit, unit2)):
+                nc.sync.dma_start(
+                    rows[PACK * place : PACK * (place + 1), :].rearrange("t (b q) -> t b q", q=8),
+                    src.rearrange("(b t q) o -> t b (q o)", t=PACK, q=8),
+                )
+            return rows
+
+        def gather_packed(table, lst, dtype, name):
+            picked = sb.tile([P, S], dtype, name=name, align_bytes=64)
+            nc.vector.tensor_copy(picked[:], table[:].indirect(lst[:]))
+            return picked
+
+        def cast_weight(raw, t, engine, name):
+            grouped = sb.tile([P, P * PACK], BF16, name=name, align_bytes=64)
+            src = raw[:].rearrange("p j (b t h i) -> p t b h j i", t=PACK, h=2, i=4)[:, t]
+            dst = grouped[:].rearrange("p (b h i j) -> p b h j i", h=2, i=4, j=PACK)
+            if engine == "v":
+                nc.vector.tensor_copy(dst, src)
+            else:
+                nc.scalar.copy(dst, src)
+            return grouped
+
+        def quantize(values, name):
+            width = values.shape[1] // PACK
+            codes = sb.tile([P, width], U32, name=name + "_codes", align_bytes=64)
+            scales = sb.tile([P, width], U8, name=name + "_scales", align_bytes=64)
+            nc.vector.quantize_mx(out=codes[:].bitcast(FP8X4), scales=scales[:], in_=values)
+            return codes, scales
+
+        def product(acc, stationary, moving, cols):
+            nc.tensor.matmul_mx(
+                out=acc,
+                lhsT=stationary[0][:].bitcast(FP8X4),
+                lhsT_scale=stationary[1][:],
+                rhs=moving[0][:, cols].bitcast(FP8X4),
+                rhs_scale=moving[1][:, cols],
+                start=True,
+                stop=True,
+            )
+
+        def window(name):
+            win = sb.tile([P, WINDOW], F32, name=name)
+            nc.vector.memset(win[:, Z:], 0.0)
+            return win
+
+        def gather_values(dst, win, lst, engine):
+            if engine == "v":
+                nc.vector.tensor_copy(dst, win[:].indirect(lst))
+            else:
+                nc.scalar.activation(dst, win[:].indirect(lst), ACT.Copy)
+
+        def quantized_weight(raw, engines, name):
+            grouped = [cast_weight(raw, t, engines[t], f"{name}_bf{t}") for t in range(PACK)]
+            return [quantize(grouped[t][:], f"{name}_q{t}") for t in range(PACK)]
+
+        everything = slice(0, Z)
+
+        gal_list = load_list(gal, "gal_list")
+        offs_list = load_list(offs, "offs_list")
+        w3_raw = load_weight(w3, "w3_raw")
+        es_table = load_scales(e_scales, "es_table")
+        factor_rows = load_factors()
+        ew_table = load_words(e_words, "ew_table")
+        xs_table = load_scales(x_scales, "xs_table")
+        w2_raw = load_weight(w2, "w2_raw")
+        cam_list = load_list(cam, "cam_list")
+        w1_raw = load_weight(w1, "w1_raw")
+        xw_table = load_words(x_words, "xw_table")
+        nn1_list = load_list(nn1, "nn1_list")
+        nn2_list = load_list(nn2, "nn2_list")
+
+        yg_win = [window(f"yg_win{t}") for t in range(PACK)]
+        sc_win = [window(f"sc_win{n}") for n in range(S // P)]
+
+        e_bytes = gather_packed(es_table, gal_list, U8, "e_bytes")
+        w3_q = quantized_weight(w3_raw, "vsss", "w3")
+        identity = sb.tile([P, P], F32, name="identity")
+        make_identity(nc, identity[:])
+        turned = psum.tile([P, P], F32, name="turned", tag="b0")
+        nc.tensor.transpose(turned[:], factor_rows[:], identity[:])
+        factors = sb.tile([P, 2 * PACK], F32, name="factors")
+        nc.scalar.copy(factors[:], turned[:, : 2 * PACK])
+        unit_col = factors[:, :PACK]
+        unit2_col = factors[:, PACK:]
+        half_unit2 = sb.tile([P, PACK], F32, name="half_unit2")
+        nc.scalar.activation(half_unit2[:], turned[:, PACK : 2 * PACK], ACT.Copy, scale=0.5)
+        e_codes = gather_packed(ew_table, gal_list, U32, "e_codes")
+        e_q = (e_codes, e_bytes)
+        x_bytes = gather_packed(xs_table, offs_list, U8, "x_bytes")
+
+        for t in range(PACK):
+            acc = psum.tile([P, Z], F32, name="yg_acc", tag=f"a{t}")
+            product(acc[:], w3_q[t], e_q, everything)
+            nc.scalar.activation(yg_win[t][:, :Z], acc[:], ACT.Copy, scale=half_unit2[:, t : t + 1])
+
+        w2_q = quantized_weight(w2_raw, "vvvv", "w2")
+        ye_acc = []
+        for t in range(PACK):
+            acc = psum.tile([P, Z], F32, name="ye_acc", tag=f"b{t}")
+            product(acc[:], w2_q[t], e_q, everything)
+            ye_acc.append(acc)
+
+        aug = sb.tile([P, PACK, Z], F32, name="aug")
+
+        def camera(t, form):
+            other = sb.tile([P, Z], F32, name=f"other{t}")
+            if form == "a":
+                nc.scalar.activation(other[:], ye_acc[t][:], ACT.Copy, scale=unit2_col[:, t : t + 1])
+                nc.vector.tensor_tensor(aug[:, t, :], yg_win[t][:].indirect(cam_list[:]), other[:], ALU.add)
+            else:
+                gather_values(other[:], yg_win[t], cam_list[:], "s")
+                nc.vector.scalar_tensor_tensor(
+                    aug[:, t, :], ye_acc[t][:], unit2_col[:, t : t + 1], other[:], ALU.mult, ALU.add
+                )
+
+        bounded = []
+
+        def probe(n):
+            acc = psum.tile([P, PACK, P], F32, name="y_acc", tag=f"a{n}")
+            for t in range(PACK):
+                product(acc[:, t, :], w1_q[t], x_q, slice(n * P, (n + 1) * P))
+            th = sb.tile([P, P, PACK], F32, name=f"tanh{n}")
+            nc.scalar.activation(th[:], acc[:].rearrange("p t n -> p n t"), ACT.Tanh)
+            bounded.append(th)
+
+        def hidden(n):
+            hid = sb.tile([P, P, PACK], BF16, name=f"probe_hid{n}", align_bytes=64)
+            nc.vector.tensor_tensor(
+                hid[:], bounded[n][:], unit_col.unsqueeze(1).to_broadcast([P, P, PACK]), ALU.mult
+            )
+            return quantize(hid[:].rearrange("p n t -> p (n t)"), f"probe_hid{n}")
+
+        camera(0, "b")
+        w1_q = quantized_weight(w1_raw, "vvvv", "w1")
+        camera(1, "b")
+        x_codes = gather_packed(xw_table, offs_list, U32, "x_codes")
+        x_q = (x_codes, x_bytes)
+        camera(2, "b")
+        camera(3, "b")
+        hid2 = sb.tile([P, Z, PACK], BF16, name="hid2", align_bytes=64)
+        woven = hid2[:].rearrange("p (c i) t -> p c t i", i=4)
+        planes = aug[:].rearrange("p t (c i) -> p c t i", i=4)
+        nc.vector.tensor_copy(woven[:, : WEAVE_ON_VECTOR // 4], planes[:, : WEAVE_ON_VECTOR // 4])
+        nc.scalar.copy(woven[:, WEAVE_ON_VECTOR // 4 :], planes[:, WEAVE_ON_VECTOR // 4 :])
+        for n in range(S // P):
+            probe(n)
+        hid2_q = quantize(hid2[:].rearrange("p e t -> p (e t)"), "hid2")
+        hid_q = [hidden(0)]
+
+        def entries(lst, first, last):
+            return lst[:, first // 16 : last // 16]
+
+        def scores(n, pieces):
+            s1 = sb.tile([P, Z], F32, name=f"s1_{n}")
+            s2 = sb.tile([P, Z], F32, name=f"s2_{n}")
+            res = sb.tile([P, Z], F32, name=f"res_{n}")
+            width = Z // pieces
+            gather_values(s2[:, :NN2_ON_VECTOR], sc_win[n], entries(nn2_list, 0, NN2_ON_VECTOR), "v")
+            for first in range(0, Z, width):
+                gather_values(s1[:, first : first + width], sc_win[n], entries(nn1_list, first, first + width), "s")
+            gather_values(s2[:, NN2_ON_VECTOR:], sc_win[n], entries(nn2_list, NN2_ON_VECTOR, Z), "s")
+            for first in range(0, Z, width):
+                cols = slice(first, first + width)
+                nc.vector.tensor_tensor(s1[:, cols], s1[:, cols], s2[:, cols], ALU.min)
+                nc.vector.scalar_tensor_tensor(res[:, cols], sc_acc[n][:, cols], 0.5, s1[:, cols], ALU.mult, ALU.add)
+                nc.sync.dma_start(out[n * P : (n + 1) * P, cols], res[:, cols])
+
+        def meet(n):
+            acc = psum.tile([P, Z], F32, name="sc_acc", tag=f"b{n}")
+            product(acc[:], hid_q[n], hid2_q, everything)
+            nc.scalar.copy(sc_win[n][:, :Z], acc[:])
+            sc_acc.append(acc)
+
+        sc_acc = []
+        tiles = S // P
+        meet(0)
+        for n in range(1, tiles):
+            hid_q.append(hidden(n))
+            meet(n)
+            scores(n - 1, 1)
+        scores(tiles - 1, 2)

@@ -18,9 +18,16 @@ ACT = mybir.ActivationFunctionType
 
 P = 128
 PACK = 4
-WINDOW = 528
+BLOCK_ROWS = 8
+LINE = 4
+STRIPE = 16
+PROBE_TILES = S // P
+HALF = Z // 2
+HALVES = (slice(0, HALF), slice(HALF, Z))
+SCORE_COLUMNS = Z + STRIPE
+W3_SLOTS_ON_VECTOR = 1
+WEAVE_ON_VECTOR = 128
 NN2_ON_VECTOR = 384
-WEAVE_ON_VECTOR = 320
 
 
 def tile_picked_yreidr_min_p_kernel(
@@ -29,6 +36,7 @@ def tile_picked_yreidr_min_p_kernel(
     nc = tc.nc
     with ExitStack() as ctx:
         sb = ctx.enter_context(tc.tile_pool(name="sb", bufs=1))
+        shared = ctx.enter_context(tc.tile_pool(name="shared", bufs=1))
         psum = ctx.enter_context(tc.psum_pool(name="psum", bufs=1))
 
         def load_list(src, name):
@@ -36,8 +44,7 @@ def tile_picked_yreidr_min_p_kernel(
             nc.sync.dma_start(lst[:], src)
             return lst
 
-        def load_weight(src, name):
-            raw = sb.tile([P, PACK, H], F32, name=name)
+        def load_weight(src, raw):
             nc.sync.dma_start(raw[:], src.rearrange("(p j) c -> p j c", j=PACK))
             return raw
 
@@ -49,34 +56,43 @@ def tile_picked_yreidr_min_p_kernel(
         def load_scales(src, name):
             table = sb.tile([P, T], U8, name=name)
             nc.vector.memset(table[:].bitcast(I32), 0)
-            for q in range(4):
-                nc.sync.dma_start(table[32 * q : 32 * q + 4, :].bitcast(I32), src[0, 4 * q : 4 * q + 4, :].bitcast(I32))
+            for quad in range(P // 32):
+                nc.sync.dma_start(
+                    table[32 * quad : 32 * quad + 4, :].bitcast(I32), src[0, 4 * quad : 4 * quad + 4, :].bitcast(I32)
+                )
             return table
 
-        def load_factors():
-            rows = sb.tile([P, P], F32, name="factor_rows")
+        def load_factor(src, name):
+            rows = sb.tile([P, P], F32, name=name)
             nc.vector.memset(rows[:], 0.0)
-            for place, src in enumerate((unit, unit2)):
-                nc.sync.dma_start(
-                    rows[PACK * place : PACK * (place + 1), :].rearrange("t (b q) -> t b q", q=8),
-                    src.rearrange("(b t q) o -> t b (q o)", t=PACK, q=8),
-                )
+            nc.sync.dma_start(
+                rows[:PACK, :].rearrange("t (b q) -> t b q", q=BLOCK_ROWS),
+                src.rearrange("(b t q) o -> t b (q o)", t=PACK, q=BLOCK_ROWS),
+            )
             return rows
 
-        def gather_packed(table, lst, dtype, name):
-            picked = sb.tile([P, S], dtype, name=name, align_bytes=64)
+        def entries(lst, first, last):
+            return lst[:, first // STRIPE : last // STRIPE]
+
+        def gather_bytes(table, lst, name):
+            picked = sb.tile([P, Z], U8, name=name, align_bytes=64)
             nc.vector.tensor_copy(picked[:], table[:].indirect(lst[:]))
             return picked
 
-        def cast_weight(raw, t, engine, name):
-            grouped = sb.tile([P, P * PACK], BF16, name=name, align_bytes=64)
-            src = raw[:].rearrange("p j (b t h i) -> p t b h j i", t=PACK, h=2, i=4)[:, t]
-            dst = grouped[:].rearrange("p (b h i j) -> p b h j i", h=2, i=4, j=PACK)
-            if engine == "v":
-                nc.vector.tensor_copy(dst, src)
-            else:
-                nc.scalar.copy(dst, src)
-            return grouped
+        def gather_words(table, lst, name):
+            picked = sb.tile([P, Z], U32, name=name, align_bytes=64)
+            for cols in HALVES:
+                nc.vector.tensor_copy(picked[:, cols], table[:].indirect(entries(lst, cols.start, cols.stop)))
+            return picked
+
+        def gather_on_scalar(dst, values, offsets):
+            nc.scalar.activation(dst, values[:].indirect(offsets), ACT.Copy)
+
+        def round_slot(copy, dst, raw, t):
+            copy(
+                dst.rearrange("p (b h i j) -> p b h j i", h=BLOCK_ROWS // LINE, i=LINE, j=PACK),
+                raw[:].rearrange("p j (b t h i) -> p t b h j i", t=PACK, h=BLOCK_ROWS // LINE, i=LINE)[:, t],
+            )
 
         def quantize(values, name):
             width = values.shape[1] // PACK
@@ -84,6 +100,24 @@ def tile_picked_yreidr_min_p_kernel(
             scales = sb.tile([P, width], U8, name=name + "_scales", align_bytes=64)
             nc.vector.quantize_mx(out=codes[:].bitcast(FP8X4), scales=scales[:], in_=values)
             return codes, scales
+
+        def quantized_slots(raw, name):
+            rounded = []
+            for t in range(PACK):
+                slot = sb.tile([P, P * PACK], BF16, name=f"{name}_bf{t}", align_bytes=64)
+                round_slot(nc.vector.tensor_copy if t < W3_SLOTS_ON_VECTOR else nc.scalar.copy, slot[:], raw, t)
+                rounded.append(slot)
+            return [quantize(rounded[t][:], f"{name}_q{t}") for t in range(PACK)]
+
+        def quantized_pairs(raw, name):
+            slots = []
+            pairs = [sb.tile([P, 2, P * PACK], BF16, name=f"{name}_bf{u}", align_bytes=64) for u in range(PACK // 2)]
+            for t in range(PACK):
+                round_slot(nc.vector.tensor_copy, pairs[t // 2][:, t % 2, :], raw, t)
+            for u, pair in enumerate(pairs):
+                codes, scales = quantize(pair[:].rearrange("p t c -> p (t c)"), f"{name}_q{u}")
+                slots.extend((codes[:, t * P : (t + 1) * P], scales[:, t * P : (t + 1) * P]) for t in range(2))
+            return slots
 
         def product(acc, stationary, moving, cols):
             nc.tensor.matmul_mx(
@@ -96,144 +130,143 @@ def tile_picked_yreidr_min_p_kernel(
                 stop=True,
             )
 
-        def window(name):
-            win = sb.tile([P, WINDOW], F32, name=name)
-            nc.vector.memset(win[:, Z:], 0.0)
-            return win
+        def score_tile(name):
+            scores = sb.tile([P, SCORE_COLUMNS], F32, name=name)
+            nc.vector.memset(scores[:, Z:], 0.0)
+            return scores
 
-        def gather_values(dst, win, lst, engine):
-            if engine == "v":
-                nc.vector.tensor_copy(dst, win[:].indirect(lst))
-            else:
-                nc.scalar.activation(dst, win[:].indirect(lst), ACT.Copy)
-
-        def quantized_weight(raw, engines, name):
-            grouped = [cast_weight(raw, t, engines[t], f"{name}_bf{t}") for t in range(PACK)]
-            return [quantize(grouped[t][:], f"{name}_q{t}") for t in range(PACK)]
-
-        everything = slice(0, Z)
-
+        w3_raw = load_weight(w3, sb.tile([P, PACK, H], F32, name="w3_raw"))
         gal_list = load_list(gal, "gal_list")
-        offs_list = load_list(offs, "offs_list")
-        w3_raw = load_weight(w3, "w3_raw")
         es_table = load_scales(e_scales, "es_table")
-        factor_rows = load_factors()
+        unit2_rows = load_factor(unit2, "unit2_rows")
         ew_table = load_words(e_words, "ew_table")
+        offs_list = load_list(offs, "offs_list")
         xs_table = load_scales(x_scales, "xs_table")
-        w2_raw = load_weight(w2, "w2_raw")
+        w2_raw = load_weight(w2, sb.tile([P, PACK, H], F32, name="w2_raw"))
         cam_list = load_list(cam, "cam_list")
-        w1_raw = load_weight(w1, "w1_raw")
+        w1_raw = load_weight(w1, shared.tile([P, PACK, H], F32, name="w1_raw", offset=0))
         xw_table = load_words(x_words, "xw_table")
+        unit_rows = load_factor(unit, "unit_rows")
         nn1_list = load_list(nn1, "nn1_list")
         nn2_list = load_list(nn2, "nn2_list")
 
-        yg_win = [window(f"yg_win{t}") for t in range(PACK)]
-        sc_win = [window(f"sc_win{n}") for n in range(S // P)]
+        yg_scaled = [sb.tile([P, Z], F32, name=f"yg_scaled{t}") for t in range(PACK)]
+        sc_tiles = [score_tile(f"sc_tile{n}") for n in range(PROBE_TILES)]
 
-        e_bytes = gather_packed(es_table, gal_list, U8, "e_bytes")
-        w3_q = quantized_weight(w3_raw, "vsss", "w3")
+        e_bytes = gather_bytes(es_table, gal_list, "e_bytes")
+        w3_q = quantized_slots(w3_raw, "w3")
+        e_q = (gather_words(ew_table, gal_list, "e_codes"), e_bytes)
+        x_bytes = gather_bytes(xs_table, offs_list, "x_bytes")
+
         identity = sb.tile([P, P], F32, name="identity")
         make_identity(nc, identity[:])
-        turned = psum.tile([P, P], F32, name="turned", tag="b0")
-        nc.tensor.transpose(turned[:], factor_rows[:], identity[:])
-        factors = sb.tile([P, 2 * PACK], F32, name="factors")
-        nc.scalar.copy(factors[:], turned[:, : 2 * PACK])
-        unit_col = factors[:, :PACK]
-        unit2_col = factors[:, PACK:]
-        half_unit2 = sb.tile([P, PACK], F32, name="half_unit2")
-        nc.scalar.activation(half_unit2[:], turned[:, PACK : 2 * PACK], ACT.Copy, scale=0.5)
-        e_codes = gather_packed(ew_table, gal_list, U32, "e_codes")
-        e_q = (e_codes, e_bytes)
-        x_bytes = gather_packed(xs_table, offs_list, U8, "x_bytes")
+        unit2_turned = psum.tile([P, P], F32, name="unit2_turned", tag="b0")
+        nc.tensor.transpose(unit2_turned[:], unit2_rows[:], identity[:])
+        unit2_col = sb.tile([P, PACK], F32, name="unit2_col")
+        nc.scalar.copy(unit2_col[:], unit2_turned[:, :PACK])
+        half_unit2_col = sb.tile([P, PACK], F32, name="half_unit2_col")
+        nc.scalar.activation(half_unit2_col[:], unit2_turned[:, :PACK], ACT.Copy, scale=0.5)
 
-        for t in range(PACK):
-            acc = psum.tile([P, Z], F32, name="yg_acc", tag=f"a{t}")
-            product(acc[:], w3_q[t], e_q, everything)
-            nc.scalar.activation(yg_win[t][:, :Z], acc[:], ACT.Copy, scale=half_unit2[:, t : t + 1])
+        yg_acc = [psum.tile([P, Z], F32, name="yg_acc", tag=f"a{t}") for t in range(PACK)]
+        for cols in HALVES:
+            for t in range(PACK):
+                product(yg_acc[t][:, cols], w3_q[t], e_q, cols)
+                nc.scalar.activation(
+                    yg_scaled[t][:, cols], yg_acc[t][:, cols], ACT.Copy, scale=half_unit2_col[:, t : t + 1]
+                )
 
-        w2_q = quantized_weight(w2_raw, "vvvv", "w2")
+        w2_q = quantized_pairs(w2_raw, "w2")
         ye_acc = []
         for t in range(PACK):
             acc = psum.tile([P, Z], F32, name="ye_acc", tag=f"b{t}")
-            product(acc[:], w2_q[t], e_q, everything)
+            product(acc[:], w2_q[t], e_q, slice(0, Z))
             ye_acc.append(acc)
 
-        aug = sb.tile([P, PACK, Z], F32, name="aug")
+        w1_q = quantized_pairs(w1_raw, "w1")
+        x_q = (gather_words(xw_table, offs_list, "x_codes"), x_bytes)
 
-        def camera(t, form):
-            other = sb.tile([P, Z], F32, name=f"other{t}")
-            if form == "a":
-                nc.scalar.activation(other[:], ye_acc[t][:], ACT.Copy, scale=unit2_col[:, t : t + 1])
-                nc.vector.tensor_tensor(aug[:, t, :], yg_win[t][:].indirect(cam_list[:]), other[:], ALU.add)
-            else:
-                gather_values(other[:], yg_win[t], cam_list[:], "s")
+        half_bytes = PACK * HALF * 4
+        hid2_rows = [shared.tile([P, PACK, HALF], F32, name=f"hid2_rows{u}", offset=u * half_bytes) for u in range(2)]
+        hid2_bf = [sb.tile([P, HALF, PACK], BF16, name=f"hid2_bf{u}", align_bytes=64) for u in range(2)]
+        hid2_q = (
+            sb.tile([P, Z], U32, name="hid2_codes", align_bytes=64),
+            sb.tile([P, Z], U8, name="hid2_scales", align_bytes=64),
+        )
+        for u, cols in enumerate(HALVES):
+            for t in range(PACK):
+                other_camera = sb.tile([P, HALF], F32, name=f"other_camera{u}_{t}")
+                gather_on_scalar(other_camera[:], yg_scaled[t], entries(cam_list, cols.start, cols.stop))
                 nc.vector.scalar_tensor_tensor(
-                    aug[:, t, :], ye_acc[t][:], unit2_col[:, t : t + 1], other[:], ALU.mult, ALU.add
+                    hid2_rows[u][:, t, :],
+                    ye_acc[t][:, cols],
+                    unit2_col[:, t : t + 1],
+                    other_camera[:],
+                    ALU.mult,
+                    ALU.add,
                 )
 
-        bounded = []
+        def weave(copy, u, first, last):
+            copy(
+                hid2_bf[u][:, first:last, :].rearrange("p (c i) t -> p c t i", i=LINE),
+                hid2_rows[u][:, :, first:last].rearrange("p t (c i) -> p c t i", i=LINE),
+            )
 
-        def probe(n):
+        def quantize_gallery(u):
+            nc.vector.quantize_mx(
+                out=hid2_q[0][:, HALVES[u]].bitcast(FP8X4),
+                scales=hid2_q[1][:, HALVES[u]],
+                in_=hid2_bf[u][:].rearrange("p e t -> p (e t)"),
+            )
+
+        weave(nc.scalar.copy, 0, 0, HALF)
+        weave(nc.vector.tensor_copy, 1, 0, WEAVE_ON_VECTOR)
+        weave(nc.scalar.copy, 1, WEAVE_ON_VECTOR, HALF)
+        quantize_gallery(0)
+
+        unit_turned = psum.tile([P, P], F32, name="unit_turned", tag="a3")
+        nc.tensor.transpose(unit_turned[:], unit_rows[:], identity[:])
+        unit_col = sb.tile([P, PACK], F32, name="unit_col")
+        nc.scalar.copy(unit_col[:], unit_turned[:, :PACK])
+
+        bounded = []
+        for n in range(PROBE_TILES):
             acc = psum.tile([P, PACK, P], F32, name="y_acc", tag=f"a{n}")
             for t in range(PACK):
                 product(acc[:, t, :], w1_q[t], x_q, slice(n * P, (n + 1) * P))
-            th = sb.tile([P, P, PACK], F32, name=f"tanh{n}")
-            nc.scalar.activation(th[:], acc[:].rearrange("p t n -> p n t"), ACT.Tanh)
-            bounded.append(th)
+            tanh = sb.tile([P, P, PACK], F32, name=f"tanh{n}")
+            nc.scalar.activation(tanh[:], acc[:].rearrange("p t n -> p n t"), ACT.Tanh)
+            bounded.append(tanh)
+        quantize_gallery(1)
 
-        def hidden(n):
-            hid = sb.tile([P, P, PACK], BF16, name=f"probe_hid{n}", align_bytes=64)
+        def meet(n):
+            hid_bf = sb.tile([P, P, PACK], BF16, name=f"hid_bf{n}", align_bytes=64)
             nc.vector.tensor_tensor(
-                hid[:], bounded[n][:], unit_col.unsqueeze(1).to_broadcast([P, P, PACK]), ALU.mult
+                hid_bf[:], bounded[n][:], unit_col[:].unsqueeze(1).to_broadcast([P, P, PACK]), ALU.mult
             )
-            return quantize(hid[:].rearrange("p n t -> p (n t)"), f"probe_hid{n}")
+            hid_q = quantize(hid_bf[:].rearrange("p n t -> p (n t)"), f"hid_q{n}")
+            acc = psum.tile([P, Z], F32, name="sc_acc", tag=f"b{n}")
+            product(acc[:], hid_q, hid2_q, slice(0, Z))
+            nc.scalar.copy(sc_tiles[n][:, :Z], acc[:])
+            return acc
 
-        camera(0, "b")
-        w1_q = quantized_weight(w1_raw, "vvvv", "w1")
-        camera(1, "b")
-        x_codes = gather_packed(xw_table, offs_list, U32, "x_codes")
-        x_q = (x_codes, x_bytes)
-        camera(2, "b")
-        camera(3, "b")
-        hid2 = sb.tile([P, Z, PACK], BF16, name="hid2", align_bytes=64)
-        woven = hid2[:].rearrange("p (c i) t -> p c t i", i=4)
-        planes = aug[:].rearrange("p t (c i) -> p c t i", i=4)
-        nc.vector.tensor_copy(woven[:, : WEAVE_ON_VECTOR // 4], planes[:, : WEAVE_ON_VECTOR // 4])
-        nc.scalar.copy(woven[:, WEAVE_ON_VECTOR // 4 :], planes[:, WEAVE_ON_VECTOR // 4 :])
-        for n in range(S // P):
-            probe(n)
-        hid2_q = quantize(hid2[:].rearrange("p e t -> p (e t)"), "hid2")
-        hid_q = [hidden(0)]
-
-        def entries(lst, first, last):
-            return lst[:, first // 16 : last // 16]
-
-        def scores(n, pieces):
+        def rerank(n, sc_acc, pieces):
             s1 = sb.tile([P, Z], F32, name=f"s1_{n}")
             s2 = sb.tile([P, Z], F32, name=f"s2_{n}")
-            res = sb.tile([P, Z], F32, name=f"res_{n}")
+            result = sb.tile([P, Z], F32, name=f"result{n}")
             width = Z // pieces
-            gather_values(s2[:, :NN2_ON_VECTOR], sc_win[n], entries(nn2_list, 0, NN2_ON_VECTOR), "v")
+            nc.vector.tensor_copy(s2[:, :NN2_ON_VECTOR], sc_tiles[n][:].indirect(entries(nn2_list, 0, NN2_ON_VECTOR)))
             for first in range(0, Z, width):
-                gather_values(s1[:, first : first + width], sc_win[n], entries(nn1_list, first, first + width), "s")
-            gather_values(s2[:, NN2_ON_VECTOR:], sc_win[n], entries(nn2_list, NN2_ON_VECTOR, Z), "s")
+                gather_on_scalar(s1[:, first : first + width], sc_tiles[n], entries(nn1_list, first, first + width))
+            gather_on_scalar(s2[:, NN2_ON_VECTOR:], sc_tiles[n], entries(nn2_list, NN2_ON_VECTOR, Z))
             for first in range(0, Z, width):
                 cols = slice(first, first + width)
                 nc.vector.tensor_tensor(s1[:, cols], s1[:, cols], s2[:, cols], ALU.min)
-                nc.vector.scalar_tensor_tensor(res[:, cols], sc_acc[n][:, cols], 0.5, s1[:, cols], ALU.mult, ALU.add)
-                nc.sync.dma_start(out[n * P : (n + 1) * P, cols], res[:, cols])
+                nc.vector.scalar_tensor_tensor(result[:, cols], sc_acc[:, cols], 0.5, s1[:, cols], ALU.mult, ALU.add)
+                nc.sync.dma_start(out[n * P : (n + 1) * P, cols], result[:, cols])
 
-        def meet(n):
-            acc = psum.tile([P, Z], F32, name="sc_acc", tag=f"b{n}")
-            product(acc[:], hid_q[n], hid2_q, everything)
-            nc.scalar.copy(sc_win[n][:, :Z], acc[:])
-            sc_acc.append(acc)
-
-        sc_acc = []
-        tiles = S // P
-        meet(0)
-        for n in range(1, tiles):
-            hid_q.append(hidden(n))
-            meet(n)
-            scores(n - 1, 1)
-        scores(tiles - 1, 2)
+        sc_acc = meet(0)
+        for n in range(1, PROBE_TILES):
+            next_acc = meet(n)
+            rerank(n - 1, sc_acc, 1)
+            sc_acc = next_acc
+        rerank(PROBE_TILES - 1, sc_acc, 2)

from contextlib import ExitStack

import concourse.mybir as mybir
from concourse.masks import make_identity

K, T, S, H, Z = 512, 2048, 512, 512, 512
FLOPS = 2 * K * H * S + 2 * 2 * K * H * Z + 2 * H * S * Z

F32 = mybir.dt.float32
BF16 = mybir.dt.bfloat16
I32 = mybir.dt.int32
U32 = mybir.dt.uint32
U16 = mybir.dt.uint16
U8 = mybir.dt.uint8
FP8X4 = mybir.dt.float8_e4m3fn_x4
ALU = mybir.AluOpType
ACT = mybir.ActivationFunctionType

P = 128
PACK = 4
BLOCK_ROWS = 8
LINE = 4
STRIPE = 16
PROBE_TILES = S // P
HALF = Z // 2
HALVES = (slice(0, HALF), slice(HALF, Z))
SCORE_COLUMNS = Z + STRIPE
W3_SLOTS_ON_VECTOR = 1
WEAVE_ON_VECTOR = 128
NN2_ON_VECTOR = 384


def tile_picked_yreidr_min_p_kernel(
    tc, x_words, x_scales, w1, e_words, e_scales, w2, w3, unit, unit2, offs, gal, cam, nn1, nn2, out
):
    nc = tc.nc
    with ExitStack() as ctx:
        sb = ctx.enter_context(tc.tile_pool(name="sb", bufs=1))
        shared = ctx.enter_context(tc.tile_pool(name="shared", bufs=1))
        psum = ctx.enter_context(tc.psum_pool(name="psum", bufs=1))

        def load_list(src, name):
            lst = sb.tile([P, src.shape[1]], U16, name=name)
            nc.sync.dma_start(lst[:], src)
            return lst

        def load_weight(src, raw):
            nc.sync.dma_start(raw[:], src.rearrange("(p j) c -> p j c", j=PACK))
            return raw

        def load_words(src, name):
            table = sb.tile([P, T], U32, name=name)
            nc.sync.dma_start(table[:].bitcast(I32), src[0].rearrange("p n t -> p (n t)").bitcast(I32))
            return table

        def load_scales(src, name):
            table = sb.tile([P, T], U8, name=name)
            nc.vector.memset(table[:].bitcast(I32), 0)
            for quad in range(P // 32):
                nc.sync.dma_start(
                    table[32 * quad : 32 * quad + 4, :].bitcast(I32), src[0, 4 * quad : 4 * quad + 4, :].bitcast(I32)
                )
            return table

        def load_factor(src, name):
            rows = sb.tile([P, P], F32, name=name)
            nc.vector.memset(rows[:], 0.0)
            nc.sync.dma_start(
                rows[:PACK, :].rearrange("t (b q) -> t b q", q=BLOCK_ROWS),
                src.rearrange("(b t q) o -> t b (q o)", t=PACK, q=BLOCK_ROWS),
            )
            return rows

        def entries(lst, first, last):
            return lst[:, first // STRIPE : last // STRIPE]

        def gather_bytes(table, lst, name):
            picked = sb.tile([P, Z], U8, name=name, align_bytes=64)
            nc.vector.tensor_copy(picked[:], table[:].indirect(lst[:]))
            return picked

        def gather_words(table, lst, name):
            picked = sb.tile([P, Z], U32, name=name, align_bytes=64)
            for cols in HALVES:
                nc.vector.tensor_copy(picked[:, cols], table[:].indirect(entries(lst, cols.start, cols.stop)))
            return picked

        def gather_on_scalar(dst, values, offsets):
            nc.scalar.activation(dst, values[:].indirect(offsets), ACT.Copy)

        def round_slot(copy, dst, raw, t):
            copy(
                dst.rearrange("p (b h i j) -> p b h j i", h=BLOCK_ROWS // LINE, i=LINE, j=PACK),
                raw[:].rearrange("p j (b t h i) -> p t b h j i", t=PACK, h=BLOCK_ROWS // LINE, i=LINE)[:, t],
            )

        def quantize(values, name):
            width = values.shape[1] // PACK
            codes = sb.tile([P, width], U32, name=name + "_codes", align_bytes=64)
            scales = sb.tile([P, width], U8, name=name + "_scales", align_bytes=64)
            nc.vector.quantize_mx(out=codes[:].bitcast(FP8X4), scales=scales[:], in_=values)
            return codes, scales

        def quantized_slots(raw, name):
            rounded = []
            for t in range(PACK):
                slot = sb.tile([P, P * PACK], BF16, name=f"{name}_bf{t}", align_bytes=64)
                round_slot(nc.vector.tensor_copy if t < W3_SLOTS_ON_VECTOR else nc.scalar.copy, slot[:], raw, t)
                rounded.append(slot)
            return [quantize(rounded[t][:], f"{name}_q{t}") for t in range(PACK)]

        def quantized_pairs(raw, name):
            slots = []
            pairs = [sb.tile([P, 2, P * PACK], BF16, name=f"{name}_bf{u}", align_bytes=64) for u in range(PACK // 2)]
            for t in range(PACK):
                round_slot(nc.vector.tensor_copy, pairs[t // 2][:, t % 2, :], raw, t)
            for u, pair in enumerate(pairs):
                codes, scales = quantize(pair[:].rearrange("p t c -> p (t c)"), f"{name}_q{u}")
                slots.extend((codes[:, t * P : (t + 1) * P], scales[:, t * P : (t + 1) * P]) for t in range(2))
            return slots

        def product(acc, stationary, moving, cols):
            nc.tensor.matmul_mx(
                out=acc,
                lhsT=stationary[0][:].bitcast(FP8X4),
                lhsT_scale=stationary[1][:],
                rhs=moving[0][:, cols].bitcast(FP8X4),
                rhs_scale=moving[1][:, cols],
                start=True,
                stop=True,
            )

        def score_tile(name):
            scores = sb.tile([P, SCORE_COLUMNS], F32, name=name)
            nc.vector.memset(scores[:, Z:], 0.0)
            return scores

        w3_raw = load_weight(w3, sb.tile([P, PACK, H], F32, name="w3_raw"))
        gal_list = load_list(gal, "gal_list")
        es_table = load_scales(e_scales, "es_table")
        unit2_rows = load_factor(unit2, "unit2_rows")
        ew_table = load_words(e_words, "ew_table")
        offs_list = load_list(offs, "offs_list")
        xs_table = load_scales(x_scales, "xs_table")
        w2_raw = load_weight(w2, sb.tile([P, PACK, H], F32, name="w2_raw"))
        cam_list = load_list(cam, "cam_list")
        w1_raw = load_weight(w1, shared.tile([P, PACK, H], F32, name="w1_raw", offset=0))
        xw_table = load_words(x_words, "xw_table")
        unit_rows = load_factor(unit, "unit_rows")
        nn1_list = load_list(nn1, "nn1_list")
        nn2_list = load_list(nn2, "nn2_list")

        yg_scaled = [sb.tile([P, Z], F32, name=f"yg_scaled{t}") for t in range(PACK)]
        sc_tiles = [score_tile(f"sc_tile{n}") for n in range(PROBE_TILES)]

        e_bytes = gather_bytes(es_table, gal_list, "e_bytes")
        w3_q = quantized_slots(w3_raw, "w3")
        e_q = (gather_words(ew_table, gal_list, "e_codes"), e_bytes)
        x_bytes = gather_bytes(xs_table, offs_list, "x_bytes")

        identity = sb.tile([P, P], F32, name="identity")
        make_identity(nc, identity[:])
        unit2_turned = psum.tile([P, P], F32, name="unit2_turned", tag="b0")
        nc.tensor.transpose(unit2_turned[:], unit2_rows[:], identity[:])
        unit2_col = sb.tile([P, PACK], F32, name="unit2_col")
        nc.scalar.copy(unit2_col[:], unit2_turned[:, :PACK])
        half_unit2_col = sb.tile([P, PACK], F32, name="half_unit2_col")
        nc.scalar.activation(half_unit2_col[:], unit2_turned[:, :PACK], ACT.Copy, scale=0.5)

        yg_acc = [psum.tile([P, Z], F32, name="yg_acc", tag=f"a{t}") for t in range(PACK)]
        for cols in HALVES:
            for t in range(PACK):
                product(yg_acc[t][:, cols], w3_q[t], e_q, cols)
                nc.scalar.activation(
                    yg_scaled[t][:, cols], yg_acc[t][:, cols], ACT.Copy, scale=half_unit2_col[:, t : t + 1]
                )

        w2_q = quantized_pairs(w2_raw, "w2")
        ye_acc = []
        for t in range(PACK):
            acc = psum.tile([P, Z], F32, name="ye_acc", tag=f"b{t}")
            product(acc[:], w2_q[t], e_q, slice(0, Z))
            ye_acc.append(acc)

        w1_q = quantized_pairs(w1_raw, "w1")
        x_q = (gather_words(xw_table, offs_list, "x_codes"), x_bytes)

        half_bytes = PACK * HALF * 4
        hid2_rows = [shared.tile([P, PACK, HALF], F32, name=f"hid2_rows{u}", offset=u * half_bytes) for u in range(2)]
        hid2_bf = [sb.tile([P, HALF, PACK], BF16, name=f"hid2_bf{u}", align_bytes=64) for u in range(2)]
        hid2_q = (
            sb.tile([P, Z], U32, name="hid2_codes", align_bytes=64),
            sb.tile([P, Z], U8, name="hid2_scales", align_bytes=64),
        )
        for u, cols in enumerate(HALVES):
            for t in range(PACK):
                other_camera = sb.tile([P, HALF], F32, name=f"other_camera{u}_{t}")
                gather_on_scalar(other_camera[:], yg_scaled[t], entries(cam_list, cols.start, cols.stop))
                nc.vector.scalar_tensor_tensor(
                    hid2_rows[u][:, t, :],
                    ye_acc[t][:, cols],
                    unit2_col[:, t : t + 1],
                    other_camera[:],
                    ALU.mult,
                    ALU.add,
                )

        def weave(copy, u, first, last):
            copy(
                hid2_bf[u][:, first:last, :].rearrange("p (c i) t -> p c t i", i=LINE),
                hid2_rows[u][:, :, first:last].rearrange("p t (c i) -> p c t i", i=LINE),
            )

        def quantize_gallery(u):
            nc.vector.quantize_mx(
                out=hid2_q[0][:, HALVES[u]].bitcast(FP8X4),
                scales=hid2_q[1][:, HALVES[u]],
                in_=hid2_bf[u][:].rearrange("p e t -> p (e t)"),
            )

        weave(nc.scalar.copy, 0, 0, HALF)
        weave(nc.vector.tensor_copy, 1, 0, WEAVE_ON_VECTOR)
        weave(nc.scalar.copy, 1, WEAVE_ON_VECTOR, HALF)
        quantize_gallery(0)

        unit_turned = psum.tile([P, P], F32, name="unit_turned", tag="a3")
        nc.tensor.transpose(unit_turned[:], unit_rows[:], identity[:])
        unit_col = sb.tile([P, PACK], F32, name="unit_col")
        nc.scalar.copy(unit_col[:], unit_turned[:, :PACK])

        bounded = []
        for n in range(PROBE_TILES):
            acc = psum.tile([P, PACK, P], F32, name="y_acc", tag=f"a{n}")
            for t in range(PACK):
                product(acc[:, t, :], w1_q[t], x_q, slice(n * P, (n + 1) * P))
            tanh = sb.tile([P, P, PACK], F32, name=f"tanh{n}")
            nc.scalar.activation(tanh[:], acc[:].rearrange("p t n -> p n t"), ACT.Tanh)
            bounded.append(tanh)
        quantize_gallery(1)

        def meet(n):
            hid_bf = sb.tile([P, P, PACK], BF16, name=f"hid_bf{n}", align_bytes=64)
            nc.vector.tensor_tensor(
                hid_bf[:], bounded[n][:], unit_col[:].unsqueeze(1).to_broadcast([P, P, PACK]), ALU.mult
            )
            hid_q = quantize(hid_bf[:].rearrange("p n t -> p (n t)"), f"hid_q{n}")
            acc = psum.tile([P, Z], F32, name="sc_acc", tag=f"b{n}")
            product(acc[:], hid_q, hid2_q, slice(0, Z))
            nc.scalar.copy(sc_tiles[n][:, :Z], acc[:])
            return acc

        def rerank(n, sc_acc, pieces):
            s1 = sb.tile([P, Z], F32, name=f"s1_{n}")
            s2 = sb.tile([P, Z], F32, name=f"s2_{n}")
            result = sb.tile([P, Z], F32, name=f"result{n}")
            width = Z // pieces
            nc.vector.tensor_copy(s2[:, :NN2_ON_VECTOR], sc_tiles[n][:].indirect(entries(nn2_list, 0, NN2_ON_VECTOR)))
            for first in range(0, Z, width):
                gather_on_scalar(s1[:, first : first + width], sc_tiles[n], entries(nn1_list, first, first + width))
            gather_on_scalar(s2[:, NN2_ON_VECTOR:], sc_tiles[n], entries(nn2_list, NN2_ON_VECTOR, Z))
            for first in range(0, Z, width):
                cols = slice(first, first + width)
                nc.vector.tensor_tensor(s1[:, cols], s1[:, cols], s2[:, cols], ALU.min)
                nc.vector.scalar_tensor_tensor(result[:, cols], sc_acc[:, cols], 0.5, s1[:, cols], ALU.mult, ALU.add)
                nc.sync.dma_start(out[n * P : (n + 1) * P, cols], result[:, cols])

        sc_acc = meet(0)
        for n in range(1, PROBE_TILES):
            next_acc = meet(n)
            rerank(n - 1, sc_acc, 1)
            sc_acc = next_acc
        rerank(PROBE_TILES - 1, sc_acc, 2)
